import numpy as np
import ml_dtypes


def mxq(x, axis, fmt="e4m3"):
    dtype, down = {"e4m3": (ml_dtypes.float8_e4m3fn, 7), "e5m2": (ml_dtypes.float8_e5m2, 14)}[fmt]
    v = np.moveaxis(np.asarray(x, np.float32).astype(ml_dtypes.bfloat16).astype(np.float64), axis, -1)
    blocks = v.reshape(v.shape[:-1] + (-1, 32))
    amax = np.abs(blocks).max(-1, keepdims=True)
    byte = np.maximum(np.where(amax > 0, np.frexp(amax)[1] - 1 + 127, 0) - down, 1)
    scale = np.exp2(byte - 127.0)
    codes = (blocks / scale).astype(np.float32).astype(dtype).astype(np.float64)
    return np.moveaxis((codes * scale).reshape(v.shape), -1, axis)


WIDE = False


def mx_kscale(k):
    if not WIDE:
        return np.ones(k)
    levels = np.array([30, -30])
    if k % 512:
        return np.exp2(np.random.permutation(np.resize(levels, k // 32))).repeat(32)
    a = np.empty((k // 512, 16))
    for p in range(k // 512):
        a[p, :8] = np.random.permutation(np.resize(levels, 8))
        for g in range(8):
            far = levels[np.abs(levels - a[p, g]) >= 10]
            a[p, g + 8] = far[np.random.randint(len(far))]
    return np.exp2(a.ravel()).repeat(32)


def f64(x):
    return np.asarray(x).astype(np.float64)


def striped(idx):
    return np.tile(np.asarray(idx).reshape(-1, 16).T, (8, 1)).astype(np.uint16)


def unstriped(offs):
    return offs[:16].T.reshape(-1).astype(np.int64)


E2M1 = np.array([0.0, 0.5, 1.0, 1.5, 2.0, 3.0, 4.0, 6.0, -0.0, -0.5, -1.0, -1.5, -2.0, -3.0, -4.0, -6.0])


def pack_weight(w, fmt):
    k, n = w.shape
    w = f64(np.asarray(w, np.float32).astype(ml_dtypes.bfloat16)).reshape(k // 32, 32, n)
    amax = np.abs(w).max(1)
    if fmt in ("e4m3", "e5m2"):
        byte = np.frexp(amax)[1] - 1 + 127 - (7 if fmt == "e4m3" else 14)
    else:
        mant, ex = np.frexp(amax / 6.0)
        byte = np.where(mant > 0.5, ex, ex - 1) + 127
    byte = np.clip(np.where(amax > 0, byte, 1), 1, 254)
    scaled = (w * np.exp2(127.0 - byte)[:, None, :]).reshape(k, n).astype(np.float32)
    by_word = np.ascontiguousarray(scaled.reshape(k // 512, 128, 4, n).transpose(0, 1, 3, 2))
    if fmt in ("e4m3", "e5m2"):
        words = by_word.astype(ml_dtypes.float8_e4m3fn if fmt == "e4m3" else ml_dtypes.float8_e5m2).view(np.uint8)
    else:
        c = by_word.astype(ml_dtypes.float4_e2m1fn).view(np.uint8) & 0xF
        words = (c[..., 0::2] | (c[..., 1::2] << 4)).reshape(k // 512, 128, 2 * n)
    return np.ascontiguousarray(words), np.ascontiguousarray(byte.astype(np.uint8).reshape(k // 512, 16, n))


def unpack_weight(words, scales, fmt):
    g, _, n = scales.shape
    words = np.ascontiguousarray(words).reshape(g, 128, n, -1)
    if fmt in ("e4m3", "e5m2"):
        vals = words.view(ml_dtypes.float8_e4m3fn if fmt == "e4m3" else ml_dtypes.float8_e5m2).astype(np.float64)
    else:
        nib = np.empty((g, 128, n, 4), np.uint8)
        nib[..., 0::2] = words & 0xF
        nib[..., 1::2] = words >> 4
        vals = E2M1[nib]
    vals = vals * np.repeat(np.exp2(scales.astype(np.float64) - 127.0), 8, axis=1)[..., None]
    return vals.transpose(0, 1, 3, 2).reshape(g * 512, n)


K, T, J, R, V, M, Q, O, D, N, U = 512, 1024, 256, 512, 1024, 512, 128, 128, 256, 256, 128


def setup_inputs():
    n = np.random.standard_normal
    idx = np.random.permutation(V)[:R]
    idx2 = np.random.permutation(T)[:J]
    idx3 = np.random.permutation(J)[:O]
    idx4 = np.random.permutation(J)[:O]
    idx5 = np.random.permutation(D)[:U]
    idx6 = np.random.permutation(D)[:U]
    fk = mx_kscale(K)
    fm = mx_kscale(M)
    fr = mx_kscale(R)
    xtp = pack_weight(n((K, T)) / fk[:, None], "e2m1")
    wtp = pack_weight(n((K, V)) * 1 / np.sqrt(K) * fk[:, None], "e4m3")
    xcp = pack_weight(n((M, Q)) / fm[:, None], "e4m3")
    wgp = pack_weight(n((M, R)) * 1 / np.sqrt(M) * fm[:, None] * fr, "e5m2")
    wbp = pack_weight(n((R, N)) * 1 / np.sqrt(R) / fr[:, None], "e2m1")
    return {
        "xt_words": xtp[0],
        "xt_scales": xtp[1],
        "wt_words": wtp[0],
        "wt_scales": wtp[1],
        "xc_words": xcp[0],
        "xc_scales": xcp[1],
        "wg_words": wgp[0],
        "wg_scales": wgp[1],
        "wb_words": wbp[0],
        "wb_scales": wbp[1],
        "so": (np.random.uniform(0.5, 1.6, (N, 1))).astype(np.float32),
        "offs": striped(idx),
        "offs2": striped(idx2),
        "offs3": striped(idx3),
        "offs4": striped(idx4),
        "offs5": striped(idx5),
        "offs6": striped(idx6),
    }


def reference(xt_words, xt_scales, wt_words, wt_scales, xc_words, xc_scales, wg_words, wg_scales, wb_words, wb_scales, so, offs, offs2, offs3, offs4, offs5, offs6):
    idx = unstriped(offs)
    idx2 = unstriped(offs2)
    idx3 = unstriped(offs3)
    idx4 = unstriped(offs4)
    idx5 = unstriped(offs5)
    idx6 = unstriped(offs6)
    xtu = unpack_weight(xt_words, xt_scales, "e2m1")
    wtu = unpack_weight(wt_words, wt_scales, "e4m3")
    xcu = unpack_weight(xc_words, xc_scales, "e4m3")
    wgu = unpack_weight(wg_words, wg_scales, "e5m2")
    wbu = unpack_weight(wb_words, wb_scales, "e2m1")
    wtidxg = wtu[:, idx]
    xtidx2g = xtu[:, idx2]
    a = wtidxg.T @ xtidx2g
    g0 = wgu.T @ xcu
    ga = g0[:, 0:1]
    gb = g0[:, 64:65]
    h1 = np.maximum(a[:, idx3] * ga, a[:, idx4] * gb)
    hid = np.concatenate([h1, g0], axis=1)
    hidq = mxq(hid, 0, "e5m2")
    p = wbu.T @ hidq
    y = p[:, idx5] - p[:, idx6] * f64(so)
    return y

@@ -1,0 +1,151 @@
+from contextlib import ExitStack
+
+import concourse.mybir as mybir
+
+K, T, J, R, V, M, Q, O, D, N, U = 512, 1024, 256, 512, 1024, 512, 128, 128, 256, 256, 128
+FLOPS = 2 * K * R * J + 2 * M * R * Q + 2 * R * N * D
+
+F32 = mybir.dt.float32
+BF16 = mybir.dt.bfloat16
+I32 = mybir.dt.int32
+U32 = mybir.dt.uint32
+U16 = mybir.dt.uint16
+U8 = mybir.dt.uint8
+E4M3X4 = mybir.dt.float8_e4m3fn_x4
+E5M2X4 = mybir.dt.float8_e5m2_x4
+E2M1X4 = mybir.dt.float4_e2m1fn_x4
+COPY = mybir.ActivationFunctionType.Copy
+ALU = mybir.AluOpType
+
+P = 128
+PACK = 4
+
+
+def tile_list_ctxbeside_chosen_one_weighedout_kernel(
+    tc, xt_words, xt_scales, wt_words, wt_scales, xc_words, xc_scales, wg_words, wg_scales,
+    wb_words, wb_scales, so, offs, offs2, offs3, offs4, offs5, offs6, out,
+):
+    nc = tc.nc
+    with ExitStack() as ctx:
+        sb = ctx.enter_context(tc.tile_pool(name="sb", bufs=1))
+        ps = ctx.enter_context(tc.psum_pool(name="ps", bufs=1))
+
+        def sbt(name, shape, dtype):
+            return sb.tile(shape, dtype, name=name, align_bytes=64)
+
+        lists = [sb.tile([P, n // 16], U16, name="list%d" % i) for i, n in enumerate((R, J, O, O, U, U))]
+        xt_w = sbt("xt_w", [P, T], U16)
+        wt_w = sbt("wt_w", [P, V], U32)
+        xc_w = sbt("xc_w", [P, Q], U32)
+        wg_w = sbt("wg_w", [P, R], U32)
+        wb_w = sbt("wb_w", [P, N], U16)
+        xt_s = sbt("xt_s", [P, T], U8)
+        wt_s = sbt("wt_s", [P, V], U8)
+        xc_s = sbt("xc_s", [P, Q], U8)
+        wg_s = sbt("wg_s", [P, R], U8)
+        wb_s = sbt("wb_s", [P, N], U8)
+        so_t = sbt("so_t", [P, 2], F32)
+
+        def load_words(queue, tile, words):
+            queue.dma_start(out=tile[:].bitcast(I32), in_=words.bitcast(I32))
+
+        def load_rows(queue, plane, scales, quads):
+            for q in quads:
+                queue.dma_start(out=plane[:].bitcast(I32)[32 * q : 32 * q + 4, :], in_=scales[0].bitcast(I32)[4 * q : 4 * q + 4, :])
+
+        for plane in (wt_s, xc_s, wg_s, xt_s, wb_s):
+            nc.vector.memset(plane[:].bitcast(I32), 0)
+        load_words(nc.sync, wt_w, wt_words[0].rearrange("p n t -> p (n t)"))
+        nc.sync.dma_start(lists[0][:], offs)
+        load_rows(nc.sync, wt_s, wt_scales, (0, 1, 2, 3,))
+        load_words(nc.sync, wg_w, wg_words[0].rearrange("p n t -> p (n t)"))
+        load_words(nc.sync, xc_w, xc_words[0].rearrange("p n t -> p (n t)"))
+        load_rows(nc.sync, wg_s, wg_scales, (0, 1, 2, 3,))
+        nc.sync.dma_start(lists[1][:], offs2)
+        load_words(nc.sync, xt_w, xt_words[0])
+        load_rows(nc.sync, xt_s, xt_scales, (0, 1, 2, 3,))
+        load_rows(nc.gpsimd, xc_s, xc_scales, (0, 1, 2, 3,))
+        nc.sync.dma_start(lists[2][:], offs3)
+        nc.sync.dma_start(lists[3][:], offs4)
+        load_words(nc.sync, wb_w, wb_words[0])
+        load_rows(nc.sync, wb_s, wb_scales, (0, 1, 2, 3,))
+        nc.sync.dma_start(lists[4][:], offs5)
+        nc.sync.dma_start(lists[5][:], offs6)
+        with nc.allow_non_contiguous_dma(reason="one weight for each partition and half"):
+            nc.gpsimd.dma_start(out=so_t[:], in_=so.rearrange("(h p) o -> p (h o)", h=2))
+
+
+        xt_gs = sbt("xt_gs", [P, J], U8)
+        xt_gw = sbt("xt_gw", [P, J], U16)
+        wt_gs = sbt("wt_gs", [P, R], U8)
+        wt_gw = sbt("wt_gw", [P, R], U32)
+        dealt = "p (t m) -> p m t"
+        nc.vector.tensor_copy(out=wt_gs[:].rearrange(dealt, t=PACK), in_=wt_s[:].indirect(lists[0][:]))
+        nc.vector.tensor_copy(out=wt_gw[:].rearrange(dealt, t=PACK), in_=wt_w[:].indirect(lists[0][:]))
+        wg_ps = sbt("wg_ps", [P, R], U8)
+        nc.vector.tensor_copy(out=wg_ps[:].rearrange(dealt, t=PACK), in_=wg_s[:].rearrange("p (m t) -> p m t", t=PACK))
+        nc.vector.tensor_copy(out=xt_gw[:], in_=xt_w[:].indirect(lists[1][:]))
+        nc.vector.tensor_copy(out=xt_gs[:], in_=xt_s[:].indirect(lists[1][:]))
+
+        wg_pw = sbt("wg_pw", [P, R], U32)
+        nc.scalar.copy(out=wg_pw[:].rearrange(dealt, t=PACK), in_=wg_w[:].rearrange("p (m t) -> p m t", t=PACK))
+        g_ps = ps.tile([P, PACK, Q], F32, name="g_ps")
+        for t in range(PACK):
+            cols = slice(P * t, P * (t + 1))
+            nc.tensor.matmul_mx(out=g_ps[:, t, :], lhsT=wg_pw[:, cols].bitcast(E5M2X4), lhsT_scale=wg_ps[:, cols],
+                                rhs=xc_w[:].bitcast(E4M3X4), rhs_scale=xc_s[:], start=True, stop=True)
+        gains = sbt("gains", [P, PACK, 2], F32)
+        nc.scalar.activation(out=gains[:], in_=g_ps[:, :, 0:Q:64], func=COPY)
+        hid_g = sbt("hid_g", [P, Q, PACK], BF16)
+        nc.scalar.copy(out=hid_g[:], in_=g_ps[:].rearrange("p t q -> p q t"))
+
+        a_sb = []
+        for t in range(PACK):
+            cols = slice(P * t, P * (t + 1))
+            a_ps = ps.tile([P, J], F32, name="a_ps%d" % t)
+            nc.tensor.matmul_mx(out=a_ps[:], lhsT=wt_gw[:, cols].bitcast(E4M3X4), lhsT_scale=wt_gs[:, cols],
+                                rhs=xt_gw[:].bitcast(E2M1X4), rhs_scale=xt_gs[:], start=True, stop=True)
+            a_t = sbt("a_sb%d" % t, [P, J], F32)
+            nc.vector.tensor_copy(out=a_t[:], in_=a_ps[:])
+            a_sb.append(a_t)
+
+        p_sb = [sbt("p_sb%d" % h, [P, D], F32) for h in range(2)]
+
+        def second_stage(hid, name, banks, cols, engines):
+            codes = sbt(name + "_codes", [P, P], U32)
+            scales = sbt(name + "_scales", [P, P], U8)
+            nc.vector.quantize_mx(out=codes[:].bitcast(E5M2X4), scales=scales[:], in_=hid[:].rearrange("p d t -> p (d t)"))
+            for h in range(2):
+                rows = slice(P * h, P * (h + 1))
+                nc.tensor.matmul_mx(out=banks[h], lhsT=wb_w[:, rows].bitcast(E2M1X4), lhsT_scale=wb_s[:, rows],
+                                    rhs=codes[:].bitcast(E5M2X4), rhs_scale=scales[:], start=True, stop=True)
+            for h in range(2):
+                engines[h](out=p_sb[h][:, cols], in_=banks[h])
+
+        pg_ps = ps.tile([P, 2, Q], F32, name="pg_ps")
+        second_stage(hid_g, "hg", [pg_ps[:, 0, :], pg_ps[:, 1, :]], slice(O, D), [nc.vector.tensor_copy, nc.vector.tensor_copy])
+
+        hid_h = sbt("hid_h", [P, O, PACK], BF16)
+        for u in range(2):
+            pa = sbt("pa%d" % u, [P, 2, O], F32)
+            pb = sbt("pb%d" % u, [P, 2, O], F32)
+            for e in range(2):
+                t = 2 * u + e
+                nc.scalar.activation(out=pa[:, e, :], in_=a_sb[t][:].indirect(lists[2][:]), func=COPY, scale=gains[:, t, 0:1])
+                nc.scalar.activation(out=pb[:, e, :], in_=a_sb[t][:].indirect(lists[3][:]), func=COPY, scale=gains[:, t, 1:2])
+            nc.vector.tensor_tensor(out=hid_h[:, :, 2 * u : 2 * u + 2], in0=pa[:].rearrange("p e o -> p o e"),
+                                    in1=pb[:].rearrange("p e o -> p o e"), op=ALU.max)
+
+        ph_ps = [ps.tile([P, O], F32, name="ph_ps%d" % h) for h in range(2)]
+        second_stage(hid_h, "hh", [ph_ps[0][:], ph_ps[1][:]], slice(0, O), [nc.vector.tensor_copy, nc.scalar.copy])
+
+        first = [sbt("first%d" % h, [P, U], F32) for h in range(2)]
+        second = [sbt("second%d" % h, [P, U], F32) for h in range(2)]
+        for h in range(2):
+            nc.vector.tensor_copy(out=first[h][:], in_=p_sb[h][:].indirect(lists[4][:]))
+        for h in (1, 0):
+            nc.scalar.activation(out=second[h][:], in_=p_sb[h][:].indirect(lists[5][:]), func=COPY, scale=so_t[:, h : h + 1])
+        for h in (1, 0):
+            y = sbt("y%d" % h, [P, U], F32)
+            nc.vector.tensor_tensor(out=y[:], in0=first[h][:], in1=second[h][:], op=ALU.subtract)
+            nc.sync.dma_start(out=out[P * h : P * (h + 1), :], in_=y[:])

@@ -40,52 +40,65 @@ def tile_list_ctxbeside_chosen_one_weighedout_kernel(
         wg_w = sbt("wg_w", [P, R], U32)
         wb_w = sbt("wb_w", [P, N], U16)
         xt_s = sbt("xt_s", [P, T], U8)
-        wt_s = sbt("wt_s", [P, V], U8)
-        xc_s = sbt("xc_s", [P, Q], U8)
-        wg_s = sbt("wg_s", [P, R], U8)
+        wt_s = sb.tile([P, V], U8, name="wt_s", tag="shared2", align_bytes=64)
+        xc_s = sbt("xc_s", [P, 2, Q], U8)
+        wg_s = sb.tile([P, 2, R], U8, name="wg_s", tag="shared", align_bytes=64)
         wb_s = sbt("wb_s", [P, N], U8)
         so_t = sbt("so_t", [P, 2], F32)
 
         def load_words(queue, tile, words):
             queue.dma_start(out=tile[:].bitcast(I32), in_=words.bitcast(I32))
 
+        def load_halves(queue, plane, scales):
+            rows = scales[0].bitcast(I32).rearrange("(h q r) w -> q r h w", h=2, q=2)
+            for q in range(2):
+                queue.dma_start(out=plane[:].bitcast(I32)[32 * q : 32 * q + 4, :, :], in_=rows[q])
+
         def load_rows(queue, plane, scales, quads):
             for q in quads:
                 queue.dma_start(out=plane[:].bitcast(I32)[32 * q : 32 * q + 4, :], in_=scales[0].bitcast(I32)[4 * q : 4 * q + 4, :])
 
-        for plane in (wt_s, xc_s, wg_s, xt_s, wb_s):
-            nc.vector.memset(plane[:].bitcast(I32), 0)
-        load_words(nc.sync, wt_w, wt_words[0].rearrange("p n t -> p (n t)"))
-        nc.sync.dma_start(lists[0][:], offs)
-        load_rows(nc.sync, wt_s, wt_scales, (0, 1, 2, 3,))
-        load_words(nc.sync, wg_w, wg_words[0].rearrange("p n t -> p (n t)"))
-        load_words(nc.sync, xc_w, xc_words[0].rearrange("p n t -> p (n t)"))
-        load_rows(nc.sync, wg_s, wg_scales, (0, 1, 2, 3,))
+        nc.vector.memset(xt_s[:].bitcast(I32)[:, 0:128], 0)
+        nc.gpsimd.memset(xt_s[:].bitcast(I32)[:, 128:256], 0)
+        nc.vector.memset(wg_s[:].bitcast(I32), 0)
+        nc.gpsimd.memset(xc_s[:].bitcast(I32), 0)
+        nc.gpsimd.memset(wt_s[:].bitcast(I32)[:, 128:256], 0)
+        nc.vector.memset(wt_s[:].bitcast(I32)[:, 0:128], 0)
+        nc.vector.memset(wb_s[:].bitcast(I32), 0)
         nc.sync.dma_start(lists[1][:], offs2)
+        nc.sync.dma_start(lists[0][:], offs)
         load_words(nc.sync, xt_w, xt_words[0])
         load_rows(nc.sync, xt_s, xt_scales, (0, 1, 2, 3,))
-        load_rows(nc.gpsimd, xc_s, xc_scales, (0, 1, 2, 3,))
+        load_words(nc.sync, wt_w, wt_words[0].rearrange("p n t -> p (n t)"))
+        load_halves(nc.sync, wg_s, wg_scales)
+        load_halves(nc.sync, xc_s, xc_scales)
+        load_rows(nc.sync, wt_s, wt_scales, (0, 1, 2, 3,))
+        load_words(nc.gpsimd, xc_w, xc_words[0].rearrange("p n t -> p (n t)"))
+        load_words(nc.gpsimd, wg_w, wg_words[0].rearrange("p n t -> p (n t)"))
         nc.sync.dma_start(lists[2][:], offs3)
         nc.sync.dma_start(lists[3][:], offs4)
-        load_words(nc.sync, wb_w, wb_words[0])
+        load_words(nc.gpsimd, wb_w, wb_words[0])
         load_rows(nc.sync, wb_s, wb_scales, (0, 1, 2, 3,))
         nc.sync.dma_start(lists[4][:], offs5)
         nc.sync.dma_start(lists[5][:], offs6)
         with nc.allow_non_contiguous_dma(reason="one weight for each partition and half"):
-            nc.gpsimd.dma_start(out=so_t[:], in_=so.rearrange("(h p) o -> p (h o)", h=2))
+            nc.sync.dma_start(out=so_t[:], in_=so.rearrange("(h p) o -> p (h o)", h=2))
 
 
         xt_gs = sbt("xt_gs", [P, J], U8)
         xt_gw = sbt("xt_gw", [P, J], U16)
-        wt_gs = sbt("wt_gs", [P, R], U8)
         wt_gw = sbt("wt_gw", [P, R], U32)
         dealt = "p (t m) -> p m t"
-        nc.vector.tensor_copy(out=wt_gs[:].rearrange(dealt, t=PACK), in_=wt_s[:].indirect(lists[0][:]))
-        nc.vector.tensor_copy(out=wt_gw[:].rearrange(dealt, t=PACK), in_=wt_w[:].indirect(lists[0][:]))
-        wg_ps = sbt("wg_ps", [P, R], U8)
-        nc.vector.tensor_copy(out=wg_ps[:].rearrange(dealt, t=PACK), in_=wg_s[:].rearrange("p (m t) -> p m t", t=PACK))
         nc.vector.tensor_copy(out=xt_gw[:], in_=xt_w[:].indirect(lists[1][:]))
         nc.vector.tensor_copy(out=xt_gs[:], in_=xt_s[:].indirect(lists[1][:]))
+        nc.vector.tensor_copy(out=wt_gw[:].rearrange(dealt, t=PACK), in_=wt_w[:].indirect(lists[0][:]))
+        wg_ps = sbt("wg_ps", [P, R], U8)
+        for plane in (xc_s, wg_s):
+            nc.vector.tensor_copy(out=plane[:].bitcast(I32)[64:128, 0, :], in_=plane[:].bitcast(I32)[0:64, 1, :])
+        nc.vector.tensor_copy(out=wg_ps[:].rearrange(dealt, t=PACK), in_=wg_s[:, 0, :].rearrange("p (m t) -> p m t", t=PACK))
+        wt_gs = sb.tile([P, R], U8, name="wt_gs", tag="shared", align_bytes=64)
+        nc.vector.tensor_copy(out=wt_gs[:].rearrange(dealt, t=PACK), in_=wt_s[:].indirect(lists[0][:]))
+
 
         wg_pw = sbt("wg_pw", [P, R], U32)
         nc.scalar.copy(out=wg_pw[:].rearrange(dealt, t=PACK), in_=wg_w[:].rearrange("p (m t) -> p m t", t=PACK))
@@ -93,11 +106,10 @@ def tile_list_ctxbeside_chosen_one_weighedout_kernel(
         for t in range(PACK):
             cols = slice(P * t, P * (t + 1))
             nc.tensor.matmul_mx(out=g_ps[:, t, :], lhsT=wg_pw[:, cols].bitcast(E5M2X4), lhsT_scale=wg_ps[:, cols],
-                                rhs=xc_w[:].bitcast(E4M3X4), rhs_scale=xc_s[:], start=True, stop=True)
+                                rhs=xc_w[:].bitcast(E4M3X4), rhs_scale=xc_s[:, 0, :], start=True, stop=True)
         gains = sbt("gains", [P, PACK, 2], F32)
         nc.scalar.activation(out=gains[:], in_=g_ps[:, :, 0:Q:64], func=COPY)
-        hid_g = sbt("hid_g", [P, Q, PACK], BF16)
-        nc.scalar.copy(out=hid_g[:], in_=g_ps[:].rearrange("p t q -> p q t"))
+        hid_g = sb.tile([P, Q, PACK], BF16, name="hid_g", tag="shared2", align_bytes=64)
 
         a_sb = []
         for t in range(PACK):
@@ -106,8 +118,10 @@ def tile_list_ctxbeside_chosen_one_weighedout_kernel(
             nc.tensor.matmul_mx(out=a_ps[:], lhsT=wt_gw[:, cols].bitcast(E4M3X4), lhsT_scale=wt_gs[:, cols],
                                 rhs=xt_gw[:].bitcast(E2M1X4), rhs_scale=xt_gs[:], start=True, stop=True)
             a_t = sbt("a_sb%d" % t, [P, J], F32)
-            nc.vector.tensor_copy(out=a_t[:], in_=a_ps[:])
+            (nc.scalar.copy if t == 0 else nc.vector.tensor_copy)(out=a_t[:], in_=a_ps[:])
             a_sb.append(a_t)
+            if t == 0:
+                nc.vector.tensor_copy(out=hid_g[:], in_=g_ps[:].rearrange("p t q -> p q t"))
 
         p_sb = [sbt("p_sb%d" % h, [P, D], F32) for h in range(2)]
 
@@ -123,7 +137,6 @@ def tile_list_ctxbeside_chosen_one_weighedout_kernel(
                 engines[h](out=p_sb[h][:, cols], in_=banks[h])
 
         pg_ps = ps.tile([P, 2, Q], F32, name="pg_ps")
-        second_stage(hid_g, "hg", [pg_ps[:, 0, :], pg_ps[:, 1, :]], slice(O, D), [nc.vector.tensor_copy, nc.vector.tensor_copy])
 
         hid_h = sbt("hid_h", [P, O, PACK], BF16)
         for u in range(2):
@@ -136,6 +149,7 @@ def tile_list_ctxbeside_chosen_one_weighedout_kernel(
             nc.vector.tensor_tensor(out=hid_h[:, :, 2 * u : 2 * u + 2], in0=pa[:].rearrange("p e o -> p o e"),
                                     in1=pb[:].rearrange("p e o -> p o e"), op=ALU.max)
 
+        second_stage(hid_g, "hg", [pg_ps[:, 0, :], pg_ps[:, 1, :]], slice(O, D), [nc.scalar.copy, nc.scalar.copy])
         ph_ps = [ps.tile([P, O], F32, name="ph_ps%d" % h) for h in range(2)]
         second_stage(hid_h, "hh", [ph_ps[0][:], ph_ps[1][:]], slice(0, O), [nc.vector.tensor_copy, nc.scalar.copy])
 

@@ -1,6 +1,7 @@
 from contextlib import ExitStack
 
 import concourse.mybir as mybir
+from concourse.masks import make_identity
 
 K, T, J, R, V, M, Q, O, D, N, U = 512, 1024, 256, 512, 1024, 512, 128, 128, 256, 256, 128
 FLOPS = 2 * K * R * J + 2 * M * R * Q + 2 * R * N * D
@@ -39,74 +40,67 @@ def tile_list_ctxbeside_chosen_one_weighedout_kernel(
         xc_w = sbt("xc_w", [P, Q], U32)
         wg_w = sbt("wg_w", [P, R], U32)
         wb_w = sbt("wb_w", [P, N], U16)
-        xt_s = sbt("xt_s", [P, T], U8)
-        wt_s = sb.tile([P, V], U8, name="wt_s", tag="shared2", align_bytes=64)
-        xc_s = sbt("xc_s", [P, 2, Q], U8)
-        wg_s = sb.tile([P, 2, R], U8, name="wg_s", tag="shared", align_bytes=64)
+        xt_s = sb.tile([P, T], U8, name="xt_s", tag="shared2", align_bytes=64)
+        wt_s = sbt("wt_s", [P, V], U8)
+        xc_s = sbt("xc_s", [P, Q], U8)
+        wg_s = sbt("wg_s", [P, R], U8)
         wb_s = sbt("wb_s", [P, N], U8)
+        ident = sbt("ident", [P, P], F32)
         so_t = sbt("so_t", [P, 2], F32)
 
         def load_words(queue, tile, words):
             queue.dma_start(out=tile[:].bitcast(I32), in_=words.bitcast(I32))
 
-        def load_halves(queue, plane, scales):
-            rows = scales[0].bitcast(I32).rearrange("(h q r) w -> q r h w", h=2, q=2)
-            for q in range(2):
-                queue.dma_start(out=plane[:].bitcast(I32)[32 * q : 32 * q + 4, :, :], in_=rows[q])
-
         def load_rows(queue, plane, scales, quads):
             for q in quads:
                 queue.dma_start(out=plane[:].bitcast(I32)[32 * q : 32 * q + 4, :], in_=scales[0].bitcast(I32)[4 * q : 4 * q + 4, :])
 
-        nc.vector.memset(xt_s[:].bitcast(I32)[:, 0:128], 0)
-        nc.gpsimd.memset(xt_s[:].bitcast(I32)[:, 128:256], 0)
-        nc.vector.memset(wg_s[:].bitcast(I32), 0)
-        nc.gpsimd.memset(xc_s[:].bitcast(I32), 0)
-        nc.gpsimd.memset(wt_s[:].bitcast(I32)[:, 128:256], 0)
         nc.vector.memset(wt_s[:].bitcast(I32)[:, 0:128], 0)
+        nc.gpsimd.memset(wt_s[:].bitcast(I32)[:, 128:256], 0)
+        nc.vector.memset(wg_s[:].bitcast(I32), 0)
+        nc.vector.memset(xc_s[:].bitcast(I32), 0)
+        nc.vector.memset(xt_s[:].bitcast(I32), 0)
         nc.vector.memset(wb_s[:].bitcast(I32), 0)
-        nc.sync.dma_start(lists[1][:], offs2)
+        make_identity(nc, ident[:])
         nc.sync.dma_start(lists[0][:], offs)
+        nc.sync.dma_start(lists[1][:], offs2)
+        load_words(nc.sync, wg_w, wg_words[0].rearrange("p n t -> p (n t)"))
+        load_rows(nc.sync, wt_s, wt_scales, (0, 1, 2, 3,))
+        load_words(nc.sync, wt_w, wt_words[0].rearrange("p n t -> p (n t)"))
+        load_words(nc.sync, xc_w, xc_words[0].rearrange("p n t -> p (n t)"))
+        load_rows(nc.sync, wg_s, wg_scales, (0, 1, 2, 3,))
+        load_rows(nc.gpsimd, xc_s, xc_scales, (0, 1,))
+        load_rows(nc.sync, xc_s, xc_scales, (2, 3,))
         load_words(nc.sync, xt_w, xt_words[0])
         load_rows(nc.sync, xt_s, xt_scales, (0, 1, 2, 3,))
-        load_words(nc.sync, wt_w, wt_words[0].rearrange("p n t -> p (n t)"))
-        load_halves(nc.sync, wg_s, wg_scales)
-        load_halves(nc.sync, xc_s, xc_scales)
-        load_rows(nc.sync, wt_s, wt_scales, (0, 1, 2, 3,))
-        load_words(nc.gpsimd, xc_w, xc_words[0].rearrange("p n t -> p (n t)"))
-        load_words(nc.gpsimd, wg_w, wg_words[0].rearrange("p n t -> p (n t)"))
         nc.sync.dma_start(lists[2][:], offs3)
         nc.sync.dma_start(lists[3][:], offs4)
-        load_words(nc.gpsimd, wb_w, wb_words[0])
+        load_words(nc.sync, wb_w, wb_words[0])
         load_rows(nc.sync, wb_s, wb_scales, (0, 1, 2, 3,))
         nc.sync.dma_start(lists[4][:], offs5)
         nc.sync.dma_start(lists[5][:], offs6)
         with nc.allow_non_contiguous_dma(reason="one weight for each partition and half"):
             nc.sync.dma_start(out=so_t[:], in_=so.rearrange("(h p) o -> p (h o)", h=2))
 
-
         xt_gs = sbt("xt_gs", [P, J], U8)
         xt_gw = sbt("xt_gw", [P, J], U16)
+        wt_gs = sbt("wt_gs", [P, R], U8)
         wt_gw = sbt("wt_gw", [P, R], U32)
         dealt = "p (t m) -> p m t"
+        nc.vector.tensor_copy(out=wt_gs[:].rearrange(dealt, t=PACK), in_=wt_s[:].indirect(lists[0][:]))
+        nc.vector.tensor_copy(out=wt_gw[:].rearrange(dealt, t=PACK), in_=wt_w[:].indirect(lists[0][:]))
         nc.vector.tensor_copy(out=xt_gw[:], in_=xt_w[:].indirect(lists[1][:]))
         nc.vector.tensor_copy(out=xt_gs[:], in_=xt_s[:].indirect(lists[1][:]))
-        nc.vector.tensor_copy(out=wt_gw[:].rearrange(dealt, t=PACK), in_=wt_w[:].indirect(lists[0][:]))
-        wg_ps = sbt("wg_ps", [P, R], U8)
-        for plane in (xc_s, wg_s):
-            nc.vector.tensor_copy(out=plane[:].bitcast(I32)[64:128, 0, :], in_=plane[:].bitcast(I32)[0:64, 1, :])
-        nc.vector.tensor_copy(out=wg_ps[:].rearrange(dealt, t=PACK), in_=wg_s[:, 0, :].rearrange("p (m t) -> p m t", t=PACK))
-        wt_gs = sb.tile([P, R], U8, name="wt_gs", tag="shared", align_bytes=64)
-        nc.vector.tensor_copy(out=wt_gs[:].rearrange(dealt, t=PACK), in_=wt_s[:].indirect(lists[0][:]))
 
-
-        wg_pw = sbt("wg_pw", [P, R], U32)
-        nc.scalar.copy(out=wg_pw[:].rearrange(dealt, t=PACK), in_=wg_w[:].rearrange("p (m t) -> p m t", t=PACK))
+        gt_ps = ps.tile([P, R], F32, name="gt_ps", tag="bank0")
+        nc.tensor.matmul_mx(out=gt_ps[:], lhsT=xc_w[:].bitcast(E4M3X4), lhsT_scale=xc_s[:],
+                            rhs=wg_w[:].bitcast(E5M2X4), rhs_scale=wg_s[:], start=True, stop=True)
         g_ps = ps.tile([P, PACK, Q], F32, name="g_ps")
-        for t in range(PACK):
-            cols = slice(P * t, P * (t + 1))
-            nc.tensor.matmul_mx(out=g_ps[:, t, :], lhsT=wg_pw[:, cols].bitcast(E5M2X4), lhsT_scale=wg_ps[:, cols],
-                                rhs=xc_w[:].bitcast(E4M3X4), rhs_scale=xc_s[:, 0, :], start=True, stop=True)
+        for u in range(2):
+            gt = sbt("gt%d" % u, [P, 2, P], F32)
+            nc.scalar.copy(out=gt[:], in_=gt_ps[:].rearrange("q (m t) -> q t m", t=PACK)[:, 2 * u : 2 * u + 2, :])
+            for e in range(2):
+                nc.tensor.transpose(g_ps[:, 2 * u + e, :], gt[:, e, :], ident[:])
         gains = sbt("gains", [P, PACK, 2], F32)
         nc.scalar.activation(out=gains[:], in_=g_ps[:, :, 0:Q:64], func=COPY)
         hid_g = sb.tile([P, Q, PACK], BF16, name="hid_g", tag="shared2", align_bytes=64)
@@ -114,7 +108,7 @@ def tile_list_ctxbeside_chosen_one_weighedout_kernel(
         a_sb = []
         for t in range(PACK):
             cols = slice(P * t, P * (t + 1))
-            a_ps = ps.tile([P, J], F32, name="a_ps%d" % t)
+            a_ps = ps.tile([P, J], F32, name="a_ps%d" % t, tag="bank%d" % t)
             nc.tensor.matmul_mx(out=a_ps[:], lhsT=wt_gw[:, cols].bitcast(E4M3X4), lhsT_scale=wt_gs[:, cols],
                                 rhs=xt_gw[:].bitcast(E2M1X4), rhs_scale=xt_gs[:], start=True, stop=True)
             a_t = sbt("a_sb%d" % t, [P, J], F32)

@@ -57,21 +57,21 @@ def tile_list_ctxbeside_chosen_one_weighedout_kernel(
 
         nc.vector.memset(wt_s[:].bitcast(I32)[:, 0:128], 0)
         nc.gpsimd.memset(wt_s[:].bitcast(I32)[:, 128:256], 0)
+        nc.gpsimd.memset(xc_s[:].bitcast(I32), 0)
         nc.vector.memset(wg_s[:].bitcast(I32), 0)
-        nc.vector.memset(xc_s[:].bitcast(I32), 0)
         nc.vector.memset(xt_s[:].bitcast(I32), 0)
         nc.vector.memset(wb_s[:].bitcast(I32), 0)
-        make_identity(nc, ident[:])
+        nc.vector.memset(ident[:], 0.0)
         nc.sync.dma_start(lists[0][:], offs)
-        nc.sync.dma_start(lists[1][:], offs2)
+        load_words(nc.sync, xc_w, xc_words[0].rearrange("p n t -> p (n t)"))
         load_words(nc.sync, wg_w, wg_words[0].rearrange("p n t -> p (n t)"))
         load_rows(nc.sync, wt_s, wt_scales, (0, 1, 2, 3,))
         load_words(nc.sync, wt_w, wt_words[0].rearrange("p n t -> p (n t)"))
-        load_words(nc.sync, xc_w, xc_words[0].rearrange("p n t -> p (n t)"))
-        load_rows(nc.sync, wg_s, wg_scales, (0, 1, 2, 3,))
         load_rows(nc.gpsimd, xc_s, xc_scales, (0, 1,))
+        load_rows(nc.sync, wg_s, wg_scales, (0, 1, 2, 3,))
         load_rows(nc.sync, xc_s, xc_scales, (2, 3,))
         load_words(nc.sync, xt_w, xt_words[0])
+        nc.sync.dma_start(lists[1][:], offs2)
         load_rows(nc.sync, xt_s, xt_scales, (0, 1, 2, 3,))
         nc.sync.dma_start(lists[2][:], offs3)
         nc.sync.dma_start(lists[3][:], offs4)
@@ -81,6 +81,7 @@ def tile_list_ctxbeside_chosen_one_weighedout_kernel(
         nc.sync.dma_start(lists[5][:], offs6)
         with nc.allow_non_contiguous_dma(reason="one weight for each partition and half"):
             nc.sync.dma_start(out=so_t[:], in_=so.rearrange("(h p) o -> p (h o)", h=2))
+        make_identity(nc, ident[:], nomemset=True)
 
         xt_gs = sbt("xt_gs", [P, J], U8)
         xt_gw = sbt("xt_gw", [P, J], U16)

from contextlib import ExitStack

import concourse.mybir as mybir
from concourse.masks import make_identity

K, T, J, R, V, M, Q, O, D, N, U = 512, 1024, 256, 512, 1024, 512, 128, 128, 256, 256, 128
FLOPS = 2 * K * R * J + 2 * M * R * Q + 2 * R * N * D

F32 = mybir.dt.float32
BF16 = mybir.dt.bfloat16
I32 = mybir.dt.int32
U32 = mybir.dt.uint32
U16 = mybir.dt.uint16
U8 = mybir.dt.uint8
E4M3X4 = mybir.dt.float8_e4m3fn_x4
E5M2X4 = mybir.dt.float8_e5m2_x4
E2M1X4 = mybir.dt.float4_e2m1fn_x4
COPY = mybir.ActivationFunctionType.Copy
ALU = mybir.AluOpType

P = 128
PACK = 4


def tile_list_ctxbeside_chosen_one_weighedout_kernel(
    tc, xt_words, xt_scales, wt_words, wt_scales, xc_words, xc_scales, wg_words, wg_scales,
    wb_words, wb_scales, so, offs, offs2, offs3, offs4, offs5, offs6, out,
):
    nc = tc.nc
    with ExitStack() as ctx:
        sb = ctx.enter_context(tc.tile_pool(name="sb", bufs=1))
        ps = ctx.enter_context(tc.psum_pool(name="ps", bufs=1))

        def sbt(name, shape, dtype):
            return sb.tile(shape, dtype, name=name, align_bytes=64)

        lists = [sb.tile([P, n // 16], U16, name="list%d" % i) for i, n in enumerate((R, J, O, O, U, U))]
        xt_w = sbt("xt_w", [P, T], U16)
        wt_w = sbt("wt_w", [P, V], U32)
        xc_w = sbt("xc_w", [P, Q], U32)
        wg_w = sbt("wg_w", [P, R], U32)
        wb_w = sbt("wb_w", [P, N], U16)
        xt_s = sb.tile([P, T], U8, name="xt_s", tag="shared2", align_bytes=64)
        wt_s = sbt("wt_s", [P, V], U8)
        xc_s = sbt("xc_s", [P, Q], U8)
        wg_s = sbt("wg_s", [P, R], U8)
        wb_s = sbt("wb_s", [P, N], U8)
        ident = sbt("ident", [P, P], F32)
        so_t = sbt("so_t", [P, 2], F32)

        def load_words(queue, tile, words):
            queue.dma_start(out=tile[:].bitcast(I32), in_=words.bitcast(I32))

        def load_rows(queue, plane, scales, quads):
            for q in quads:
                queue.dma_start(out=plane[:].bitcast(I32)[32 * q : 32 * q + 4, :], in_=scales[0].bitcast(I32)[4 * q : 4 * q + 4, :])

        nc.vector.memset(wt_s[:].bitcast(I32)[:, 0:128], 0)
        nc.gpsimd.memset(wt_s[:].bitcast(I32)[:, 128:256], 0)
        nc.gpsimd.memset(xc_s[:].bitcast(I32), 0)
        nc.vector.memset(wg_s[:].bitcast(I32), 0)
        nc.vector.memset(xt_s[:].bitcast(I32), 0)
        nc.vector.memset(wb_s[:].bitcast(I32), 0)
        nc.vector.memset(ident[:], 0.0)
        nc.sync.dma_start(lists[0][:], offs)
        load_words(nc.sync, xc_w, xc_words[0].rearrange("p n t -> p (n t)"))
        load_words(nc.sync, wg_w, wg_words[0].rearrange("p n t -> p (n t)"))
        load_rows(nc.sync, wt_s, wt_scales, (0, 1, 2, 3,))
        load_words(nc.sync, wt_w, wt_words[0].rearrange("p n t -> p (n t)"))
        load_rows(nc.gpsimd, xc_s, xc_scales, (0, 1,))
        load_rows(nc.sync, wg_s, wg_scales, (0, 1, 2, 3,))
        load_rows(nc.sync, xc_s, xc_scales, (2, 3,))
        load_words(nc.sync, xt_w, xt_words[0])
        nc.sync.dma_start(lists[1][:], offs2)
        load_rows(nc.sync, xt_s, xt_scales, (0, 1, 2, 3,))
        nc.sync.dma_start(lists[2][:], offs3)
        nc.sync.dma_start(lists[3][:], offs4)
        load_words(nc.sync, wb_w, wb_words[0])
        load_rows(nc.sync, wb_s, wb_scales, (0, 1, 2, 3,))
        nc.sync.dma_start(lists[4][:], offs5)
        nc.sync.dma_start(lists[5][:], offs6)
        with nc.allow_non_contiguous_dma(reason="one weight for each partition and half"):
            nc.sync.dma_start(out=so_t[:], in_=so.rearrange("(h p) o -> p (h o)", h=2))
        make_identity(nc, ident[:], nomemset=True)

        xt_gs = sbt("xt_gs", [P, J], U8)
        xt_gw = sbt("xt_gw", [P, J], U16)
        wt_gs = sbt("wt_gs", [P, R], U8)
        wt_gw = sbt("wt_gw", [P, R], U32)
        dealt = "p (t m) -> p m t"
        nc.vector.tensor_copy(out=wt_gs[:].rearrange(dealt, t=PACK), in_=wt_s[:].indirect(lists[0][:]))
        nc.vector.tensor_copy(out=wt_gw[:].rearrange(dealt, t=PACK), in_=wt_w[:].indirect(lists[0][:]))
        nc.vector.tensor_copy(out=xt_gw[:], in_=xt_w[:].indirect(lists[1][:]))
        nc.vector.tensor_copy(out=xt_gs[:], in_=xt_s[:].indirect(lists[1][:]))

        gt_ps = ps.tile([P, R], F32, name="gt_ps", tag="bank0")
        nc.tensor.matmul_mx(out=gt_ps[:], lhsT=xc_w[:].bitcast(E4M3X4), lhsT_scale=xc_s[:],
                            rhs=wg_w[:].bitcast(E5M2X4), rhs_scale=wg_s[:], start=True, stop=True)
        g_ps = ps.tile([P, PACK, Q], F32, name="g_ps")
        for u in range(2):
            gt = sbt("gt%d" % u, [P, 2, P], F32)
            nc.scalar.copy(out=gt[:], in_=gt_ps[:].rearrange("q (m t) -> q t m", t=PACK)[:, 2 * u : 2 * u + 2, :])
            for e in range(2):
                nc.tensor.transpose(g_ps[:, 2 * u + e, :], gt[:, e, :], ident[:])
        gains = sbt("gains", [P, PACK, 2], F32)
        nc.scalar.activation(out=gains[:], in_=g_ps[:, :, 0:Q:64], func=COPY)
        hid_g = sb.tile([P, Q, PACK], BF16, name="hid_g", tag="shared2", align_bytes=64)

        a_sb = []
        for t in range(PACK):
            cols = slice(P * t, P * (t + 1))
            a_ps = ps.tile([P, J], F32, name="a_ps%d" % t, tag="bank%d" % t)
            nc.tensor.matmul_mx(out=a_ps[:], lhsT=wt_gw[:, cols].bitcast(E4M3X4), lhsT_scale=wt_gs[:, cols],
                                rhs=xt_gw[:].bitcast(E2M1X4), rhs_scale=xt_gs[:], start=True, stop=True)
            a_t = sbt("a_sb%d" % t, [P, J], F32)
            (nc.scalar.copy if t == 0 else nc.vector.tensor_copy)(out=a_t[:], in_=a_ps[:])
            a_sb.append(a_t)
            if t == 0:
                nc.vector.tensor_copy(out=hid_g[:], in_=g_ps[:].rearrange("p t q -> p q t"))

        p_sb = [sbt("p_sb%d" % h, [P, D], F32) for h in range(2)]

        def second_stage(hid, name, banks, cols, engines):
            codes = sbt(name + "_codes", [P, P], U32)
            scales = sbt(name + "_scales", [P, P], U8)
            nc.vector.quantize_mx(out=codes[:].bitcast(E5M2X4), scales=scales[:], in_=hid[:].rearrange("p d t -> p (d t)"))
            for h in range(2):
                rows = slice(P * h, P * (h + 1))
                nc.tensor.matmul_mx(out=banks[h], lhsT=wb_w[:, rows].bitcast(E2M1X4), lhsT_scale=wb_s[:, rows],
                                    rhs=codes[:].bitcast(E5M2X4), rhs_scale=scales[:], start=True, stop=True)
            for h in range(2):
                engines[h](out=p_sb[h][:, cols], in_=banks[h])

        pg_ps = ps.tile([P, 2, Q], F32, name="pg_ps")

        hid_h = sbt("hid_h", [P, O, PACK], BF16)
        for u in range(2):
            pa = sbt("pa%d" % u, [P, 2, O], F32)
            pb = sbt("pb%d" % u, [P, 2, O], F32)
            for e in range(2):
                t = 2 * u + e
                nc.scalar.activation(out=pa[:, e, :], in_=a_sb[t][:].indirect(lists[2][:]), func=COPY, scale=gains[:, t, 0:1])
                nc.scalar.activation(out=pb[:, e, :], in_=a_sb[t][:].indirect(lists[3][:]), func=COPY, scale=gains[:, t, 1:2])
            nc.vector.tensor_tensor(out=hid_h[:, :, 2 * u : 2 * u + 2], in0=pa[:].rearrange("p e o -> p o e"),
                                    in1=pb[:].rearrange("p e o -> p o e"), op=ALU.max)

        second_stage(hid_g, "hg", [pg_ps[:, 0, :], pg_ps[:, 1, :]], slice(O, D), [nc.scalar.copy, nc.scalar.copy])
        ph_ps = [ps.tile([P, O], F32, name="ph_ps%d" % h) for h in range(2)]
        second_stage(hid_h, "hh", [ph_ps[0][:], ph_ps[1][:]], slice(0, O), [nc.vector.tensor_copy, nc.scalar.copy])

        first = [sbt("first%d" % h, [P, U], F32) for h in range(2)]
        second = [sbt("second%d" % h, [P, U], F32) for h in range(2)]
        for h in range(2):
            nc.vector.tensor_copy(out=first[h][:], in_=p_sb[h][:].indirect(lists[4][:]))
        for h in (1, 0):
            nc.scalar.activation(out=second[h][:], in_=p_sb[h][:].indirect(lists[5][:]), func=COPY, scale=so_t[:, h : h + 1])
        for h in (1, 0):
            y = sbt("y%d" % h, [P, U], F32)
            nc.vector.tensor_tensor(out=y[:], in0=first[h][:], in1=second[h][:], op=ALU.subtract)
            nc.sync.dma_start(out=out[P * h : P * (h + 1), :], in_=y[:])
